import numpy as np
import ml_dtypes

BF16 = ml_dtypes.bfloat16


def bf(x):
    return np.asarray(x, np.float32).astype(BF16)


def f32(x):
    return np.asarray(x, np.float32)


def f64(x):
    return np.asarray(x).astype(np.float64)


def striped(idx):
    return np.tile(idx.reshape(-1, 16).T, (8, 1))


S, K, M, N, D, V = 512, 128, 128, 256, 2, 128


def setup_inputs():
    return {"table": bf(np.random.standard_normal((K, S))), "w": bf(np.random.standard_normal((D, K, M)) / np.sqrt(D * K)), "b": f32(0.5 * np.random.standard_normal((M, 1))), "offs": striped(np.random.permutation(np.tile(np.arange(S), 2))[:N])}


def reference(table, w, b, offs):
    idx = offs[:16].T.reshape(-1)
    x = f64(table)[:, idx]
    y = sum(f64(w)[t].T @ x[:, t * V : (t + 1) * V] for t in range(D))
    return np.maximum(y + f64(b), 0.0)

@@ -1,0 +1,41 @@
+import concourse.mybir as mybir
+
+BF16, F32, U16 = mybir.dt.bfloat16, mybir.dt.float32, mybir.dt.uint16
+ADD, MAX = mybir.AluOpType.add, mybir.AluOpType.max
+
+K = 128
+S = 512
+M = 128
+ENDS = 2
+EDGES = 128
+PIECE_COLS = EDGES // 16
+
+FLOPS = 2 * K * M * ENDS * EDGES
+
+
+def tile_gather_matmul_kernel(tc, table, w, b, offs, out):
+    nc = tc.nc
+    with (
+        tc.tile_pool(name="held", bufs=1) as held,
+        tc.psum_pool(name="psum", bufs=1) as psum,
+    ):
+        offsets = held.tile([128, ENDS * PIECE_COLS], U16, name="offsets")
+        nodes = held.tile([K, S], BF16, name="nodes")
+        weights = held.tile([K, ENDS, M], BF16, name="weights")
+        bias = held.tile([M, 1], F32, name="bias")
+
+        nc.sync.dma_start(offsets[:], offs)
+        nc.scalar.dma_start(nodes[:], table)
+        nc.sync.dma_start(weights[:], w.rearrange("t k m -> k t m"))
+        nc.scalar.dma_start(bias[:], b)
+
+        summed = psum.tile([M, EDGES], F32, name="summed")
+        for end in range(ENDS):
+            picked = nodes[:].indirect(offsets[:, end * PIECE_COLS : (end + 1) * PIECE_COLS])
+            nc.tensor.matmul(
+                summed[:], weights[:, end, :], picked, start=(end == 0), stop=(end == ENDS - 1)
+            )
+
+        result = held.tile([M, EDGES], F32, name="result")
+        nc.vector.tensor_scalar(result[:], summed[:], bias[:, 0:1], 0.0, ADD, MAX)
+        nc.sync.dma_start(out, result[:])

@@ -21,19 +21,20 @@ def tile_gather_matmul_kernel(tc, table, w, b, offs, out):
     ):
         offsets = held.tile([128, ENDS * PIECE_COLS], U16, name="offsets")
         nodes = held.tile([K, S], BF16, name="nodes")
-        weights = held.tile([K, ENDS, M], BF16, name="weights")
+        weights = [held.tile([K, M], BF16, name=f"weights{end}") for end in range(ENDS)]
         bias = held.tile([M, 1], F32, name="bias")
 
         nc.sync.dma_start(offsets[:], offs)
         nc.scalar.dma_start(nodes[:], table)
-        nc.sync.dma_start(weights[:], w.rearrange("t k m -> k t m"))
+        nc.sync.dma_start(weights[0][:], w[0])
+        nc.scalar.dma_start(weights[1][:], w[1])
         nc.scalar.dma_start(bias[:], b)
 
         summed = psum.tile([M, EDGES], F32, name="summed")
         for end in range(ENDS):
             picked = nodes[:].indirect(offsets[:, end * PIECE_COLS : (end + 1) * PIECE_COLS])
             nc.tensor.matmul(
-                summed[:], weights[:, end, :], picked, start=(end == 0), stop=(end == ENDS - 1)
+                summed[:], weights[end][:], picked, start=(end == 0), stop=(end == ENDS - 1)
             )
 
         result = held.tile([M, EDGES], F32, name="result")

@@ -24,9 +24,9 @@ def tile_gather_matmul_kernel(tc, table, w, b, offs, out):
         weights = [held.tile([K, M], BF16, name=f"weights{end}") for end in range(ENDS)]
         bias = held.tile([M, 1], F32, name="bias")
 
+        nc.sync.dma_start(nodes[:], table)
+        nc.scalar.dma_start(weights[0][:], w[0])
         nc.sync.dma_start(offsets[:], offs)
-        nc.scalar.dma_start(nodes[:], table)
-        nc.sync.dma_start(weights[0][:], w[0])
         nc.scalar.dma_start(weights[1][:], w[1])
         nc.scalar.dma_start(bias[:], b)
 

@@ -28,7 +28,7 @@ def tile_gather_matmul_kernel(tc, table, w, b, offs, out):
         nc.scalar.dma_start(weights[0][:], w[0])
         nc.sync.dma_start(offsets[:], offs)
         nc.scalar.dma_start(weights[1][:], w[1])
-        nc.scalar.dma_start(bias[:], b)
+        nc.sync.dma_start(bias[:], b)
 
         summed = psum.tile([M, EDGES], F32, name="summed")
         for end in range(ENDS):

@@ -9,6 +9,7 @@ M = 128
 ENDS = 2
 EDGES = 128
 PIECE_COLS = EDGES // 16
+AXI_BYTES = 256
 
 FLOPS = 2 * K * M * ENDS * EDGES
 
@@ -19,9 +20,13 @@ def tile_gather_matmul_kernel(tc, table, w, b, offs, out):
         tc.tile_pool(name="held", bufs=1) as held,
         tc.psum_pool(name="psum", bufs=1) as psum,
     ):
+        nodes = held.tile([K, S], BF16, name="nodes", align_bytes=AXI_BYTES)
+        weights = [
+            held.tile([K, M], BF16, name=f"weights{end}", align_bytes=AXI_BYTES)
+            for end in range(ENDS)
+        ]
+        result = held.tile([M, EDGES], F32, name="result", align_bytes=AXI_BYTES)
         offsets = held.tile([128, ENDS * PIECE_COLS], U16, name="offsets")
-        nodes = held.tile([K, S], BF16, name="nodes")
-        weights = [held.tile([K, M], BF16, name=f"weights{end}") for end in range(ENDS)]
         bias = held.tile([M, 1], F32, name="bias")
 
         nc.sync.dma_start(nodes[:], table)
@@ -37,6 +42,5 @@ def tile_gather_matmul_kernel(tc, table, w, b, offs, out):
                 summed[:], weights[end][:], picked, start=(end == 0), stop=(end == ENDS - 1)
             )
 
-        result = held.tile([M, EDGES], F32, name="result")
         nc.vector.tensor_scalar(result[:], summed[:], bias[:, 0:1], 0.0, ADD, MAX)
         nc.sync.dma_start(out, result[:])

@@ -9,7 +9,7 @@ M = 128
 ENDS = 2
 EDGES = 128
 PIECE_COLS = EDGES // 16
-AXI_BYTES = 256
+ROW_BYTES = 2 * S
 
 FLOPS = 2 * K * M * ENDS * EDGES
 
@@ -20,14 +20,14 @@ def tile_gather_matmul_kernel(tc, table, w, b, offs, out):
         tc.tile_pool(name="held", bufs=1) as held,
         tc.psum_pool(name="psum", bufs=1) as psum,
     ):
-        nodes = held.tile([K, S], BF16, name="nodes", align_bytes=AXI_BYTES)
+        nodes = held.tile([K, S], BF16, name="nodes", align_bytes=ROW_BYTES)
         weights = [
-            held.tile([K, M], BF16, name=f"weights{end}", align_bytes=AXI_BYTES)
+            held.tile([K, M], BF16, name=f"weights{end}", align_bytes=ROW_BYTES)
             for end in range(ENDS)
         ]
-        result = held.tile([M, EDGES], F32, name="result", align_bytes=AXI_BYTES)
-        offsets = held.tile([128, ENDS * PIECE_COLS], U16, name="offsets")
-        bias = held.tile([M, 1], F32, name="bias")
+        result = held.tile([M, EDGES], F32, name="result", align_bytes=ROW_BYTES)
+        offsets = held.tile([128, ENDS * PIECE_COLS], U16, name="offsets", align_bytes=ROW_BYTES)
+        bias = held.tile([M, 1], F32, name="bias", align_bytes=ROW_BYTES)
 
         nc.sync.dma_start(nodes[:], table)
         nc.scalar.dma_start(weights[0][:], w[0])

import concourse.mybir as mybir

BF16, F32, U16 = mybir.dt.bfloat16, mybir.dt.float32, mybir.dt.uint16
ADD, MAX = mybir.AluOpType.add, mybir.AluOpType.max

K = 128
S = 512
M = 128
ENDS = 2
EDGES = 128
PIECE_COLS = EDGES // 16
ROW_BYTES = 2 * S

FLOPS = 2 * K * M * ENDS * EDGES


def tile_gather_matmul_kernel(tc, table, w, b, offs, out):
    nc = tc.nc
    with (
        tc.tile_pool(name="held", bufs=1) as held,
        tc.psum_pool(name="psum", bufs=1) as psum,
    ):
        nodes = held.tile([K, S], BF16, name="nodes", align_bytes=ROW_BYTES)
        weights = [
            held.tile([K, M], BF16, name=f"weights{end}", align_bytes=ROW_BYTES)
            for end in range(ENDS)
        ]
        result = held.tile([M, EDGES], F32, name="result", align_bytes=ROW_BYTES)
        offsets = held.tile([128, ENDS * PIECE_COLS], U16, name="offsets", align_bytes=ROW_BYTES)
        bias = held.tile([M, 1], F32, name="bias", align_bytes=ROW_BYTES)

        nc.sync.dma_start(nodes[:], table)
        nc.scalar.dma_start(weights[0][:], w[0])
        nc.sync.dma_start(offsets[:], offs)
        nc.scalar.dma_start(weights[1][:], w[1])
        nc.sync.dma_start(bias[:], b)

        summed = psum.tile([M, EDGES], F32, name="summed")
        for end in range(ENDS):
            picked = nodes[:].indirect(offsets[:, end * PIECE_COLS : (end + 1) * PIECE_COLS])
            nc.tensor.matmul(
                summed[:], weights[end][:], picked, start=(end == 0), stop=(end == ENDS - 1)
            )

        nc.vector.tensor_scalar(result[:], summed[:], bias[:, 0:1], 0.0, ADD, MAX)
        nc.sync.dma_start(out, result[:])
